import numpy as np
import ml_dtypes

BF16 = ml_dtypes.bfloat16


def bf(x):
    return np.asarray(x, np.float32).astype(BF16)


def f32(x):
    return np.asarray(x, np.float32)


def f64(x):
    return np.asarray(x).astype(np.float64)


def striped(idx):
    return np.concatenate([l.reshape(-1, 16).T for l in idx])


def rows(idx, k):
    return np.tile(np.repeat(idx, 16, axis=0), (k // (16 * 8), 1))


def look(tab, idx):
    return np.take_along_axis(f64(tab), rows(idx, len(tab)), axis=1)


K, S, V, N, M = 512, 2048, 1024, 1024, 512


def setup_inputs():
    return {"tab": f32(np.random.standard_normal((2, K, S))), "y": f32(np.random.standard_normal((K, V))), "w": bf(np.random.standard_normal((K, M)) / np.sqrt(K)), "b": f32(0.5 * np.random.standard_normal((M, 1))), "offs": striped(np.stack([np.random.permutation(S)[:N] for _ in range(8)]))}


def reference(tab, y, w, b, offs):
    idx = np.stack([g.T.reshape(-1) for g in np.split(offs, 8)])
    x = (look(tab[0], idx) * f64(y)) * (np.tanh(look(tab[1], idx)))
    return np.maximum(f64(w).T @ x + f64(b), 0.0)

@@ -1,0 +1,92 @@
+import concourse.mybir as mybir
+from concourse.masks import make_identity
+
+F32 = mybir.dt.float32
+BF16 = mybir.dt.bfloat16
+U16 = mybir.dt.uint16
+ADD = mybir.AluOpType.add
+MAX = mybir.AluOpType.max
+MULT = mybir.AluOpType.mult
+TANH = mybir.ActivationFunctionType.Tanh
+RELU = mybir.ActivationFunctionType.Relu
+
+P = 128
+K = 512
+S = 2048
+N = 1024
+M = 512
+PIECE = 512
+BLOCKS = K // P
+PIECES = N // PIECE
+OUT_BLOCKS = M // P
+
+FLOPS = 2 * K * M * N
+
+
+def tile_lookup_vg_multanh_relu_kernel(tc, tab, y, w, b, offs, out):
+    nc = tc.nc
+    with (
+        tc.tile_pool(name="held", bufs=1) as held,
+        tc.psum_pool(name="psum", bufs=1) as psum,
+    ):
+        offsets = held.tile([P, N // 16], U16, name="offsets")
+        nc.sync.dma_start(offsets[:], offs)
+
+        bias_rows = held.tile([32, P], F32, name="bias_rows")
+        nc.vector.memset(bias_rows[:], 0.0)
+        nc.sync.dma_start(bias_rows[0:OUT_BLOCKS, :], b.rearrange("(t p) o -> t (p o)", p=P))
+
+        weights = held.tile([P, BLOCKS, M], BF16, name="weights")
+        streams, values, gates = [], [], []
+        for k in range(BLOCKS):
+            rows = slice(k * P, (k + 1) * P)
+            streams.append(held.tile([P, N], F32, name=f"stream{k}"))
+            values.append(held.tile([P, S], F32, name=f"values{k}"))
+            gates.append(held.tile([P, S], F32, name=f"gates{k}"))
+            nc.sync.dma_start(streams[k][:], y[rows, :])
+            nc.sync.dma_start(values[k][:], tab[0, rows, :])
+            nc.sync.dma_start(gates[k][:], tab[1, rows, :])
+            if k == 0:
+                nc.sync.dma_start(weights[:], w.rearrange("(k p) m -> p k m", p=P))
+
+        identity = held.tile([32, 32], F32, name="identity")
+        make_identity(nc, identity[:])
+        bias_psum = psum.tile([P, PIECE], F32, name="bias_psum", tag="acc0_0")
+        nc.tensor.matmul(bias_psum[:, 0:OUT_BLOCKS], bias_rows[:], identity[:, 0:OUT_BLOCKS], start=True, stop=True)
+        bias = held.tile([P, OUT_BLOCKS], F32, name="bias")
+        nc.vector.tensor_copy(bias[:], bias_psum[:, 0:OUT_BLOCKS])
+
+        sums = [
+            [psum.tile([P, PIECE], F32, name=f"acc{h}_{m}", tag=f"acc{h}_{m}") for m in range(OUT_BLOCKS)]
+            for h in range(PIECES)
+        ]
+
+        for k in range(BLOCKS):
+            scaled, opened = [], []
+            for h in range(PIECES):
+                entries = offsets[:, h * (PIECE // 16) : (h + 1) * (PIECE // 16)]
+                cols = slice(h * PIECE, (h + 1) * PIECE)
+                scaled.append(held.tile([P, PIECE], F32, name=f"scaled{k}_{h}"))
+                nc.vector.tensor_tensor(scaled[h][:], values[k][:].indirect(entries), streams[k][:, cols], MULT)
+                opened.append(held.tile([P, PIECE], F32, name=f"opened{k}_{h}"))
+                nc.scalar.activation(opened[h][:], gates[k][:].indirect(entries), TANH)
+            for h in range(PIECES):
+                x = held.tile([P, PIECE], BF16, name=f"x{k}_{h}")
+                nc.vector.tensor_tensor(x[:], scaled[h][:], opened[h][:], MULT)
+                for m in range(OUT_BLOCKS):
+                    nc.tensor.matmul(
+                        sums[h][m][:],
+                        weights[:, k, m * P : (m + 1) * P],
+                        x[:],
+                        start=(k == 0),
+                        stop=(k == BLOCKS - 1),
+                    )
+
+        for h in range(PIECES):
+            for m in range(OUT_BLOCKS):
+                result = held.tile([P, PIECE], F32, name=f"result{h}_{m}")
+                if m % 2 == 0:
+                    nc.scalar.activation(result[:], sums[h][m][:], RELU, bias=bias[:, m : m + 1])
+                else:
+                    nc.vector.tensor_scalar(result[:], sums[h][m][:], bias[:, m : m + 1], 0.0, ADD, MAX)
+                nc.sync.dma_start(out[m * P : (m + 1) * P, h * PIECE : (h + 1) * PIECE], result[:])

@@ -36,18 +36,18 @@ def tile_lookup_vg_multanh_relu_kernel(tc, tab, y, w, b, offs, out):
         nc.vector.memset(bias_rows[:], 0.0)
         nc.sync.dma_start(bias_rows[0:OUT_BLOCKS, :], b.rearrange("(t p) o -> t (p o)", p=P))
 
-        weights = held.tile([P, BLOCKS, M], BF16, name="weights")
-        streams, values, gates = [], [], []
+        gates, values, streams, weights = [], [], [], []
         for k in range(BLOCKS):
             rows = slice(k * P, (k + 1) * P)
-            streams.append(held.tile([P, N], F32, name=f"stream{k}"))
-            values.append(held.tile([P, S], F32, name=f"values{k}"))
             gates.append(held.tile([P, S], F32, name=f"gates{k}"))
-            nc.sync.dma_start(streams[k][:], y[rows, :])
-            nc.sync.dma_start(values[k][:], tab[0, rows, :])
+            values.append(held.tile([P, S], F32, name=f"values{k}"))
+            streams.append([held.tile([P, PIECE], F32, name=f"stream{k}_{h}") for h in range(PIECES)])
+            weights.append(held.tile([P, M], BF16, name=f"weights{k}"))
             nc.sync.dma_start(gates[k][:], tab[1, rows, :])
-            if k == 0:
-                nc.sync.dma_start(weights[:], w.rearrange("(k p) m -> p k m", p=P))
+            nc.sync.dma_start(values[k][:], tab[0, rows, :])
+            for h in range(PIECES):
+                nc.sync.dma_start(streams[k][h][:], y[rows, h * PIECE : (h + 1) * PIECE])
+            nc.sync.dma_start(weights[k][:], w[rows, :])
 
         identity = held.tile([32, 32], F32, name="identity")
         make_identity(nc, identity[:])
@@ -62,21 +62,18 @@ def tile_lookup_vg_multanh_relu_kernel(tc, tab, y, w, b, offs, out):
         ]
 
         for k in range(BLOCKS):
-            scaled, opened = [], []
             for h in range(PIECES):
                 entries = offsets[:, h * (PIECE // 16) : (h + 1) * (PIECE // 16)]
-                cols = slice(h * PIECE, (h + 1) * PIECE)
-                scaled.append(held.tile([P, PIECE], F32, name=f"scaled{k}_{h}"))
-                nc.vector.tensor_tensor(scaled[h][:], values[k][:].indirect(entries), streams[k][:, cols], MULT)
-                opened.append(held.tile([P, PIECE], F32, name=f"opened{k}_{h}"))
-                nc.scalar.activation(opened[h][:], gates[k][:].indirect(entries), TANH)
-            for h in range(PIECES):
+                opened = held.tile([P, PIECE], F32, name=f"opened{k}_{h}")
+                nc.scalar.activation(opened[:], gates[k][:].indirect(entries), TANH)
+                scaled = held.tile([P, PIECE], F32, name=f"scaled{k}_{h}")
+                nc.vector.tensor_tensor(scaled[:], values[k][:].indirect(entries), streams[k][h][:], MULT)
                 x = held.tile([P, PIECE], BF16, name=f"x{k}_{h}")
-                nc.vector.tensor_tensor(x[:], scaled[h][:], opened[h][:], MULT)
+                nc.vector.tensor_tensor(x[:], scaled[:], opened[:], MULT)
                 for m in range(OUT_BLOCKS):
                     nc.tensor.matmul(
                         sums[h][m][:],
-                        weights[:, k, m * P : (m + 1) * P],
+                        weights[k][:, m * P : (m + 1) * P],
                         x[:],
                         start=(k == 0),
                         stop=(k == BLOCKS - 1),
@@ -85,7 +82,7 @@ def tile_lookup_vg_multanh_relu_kernel(tc, tab, y, w, b, offs, out):
         for h in range(PIECES):
             for m in range(OUT_BLOCKS):
                 result = held.tile([P, PIECE], F32, name=f"result{h}_{m}")
-                if m % 2 == 0:
+                if h == 0 or m % 2 == 1:
                     nc.scalar.activation(result[:], sums[h][m][:], RELU, bias=bias[:, m : m + 1])
                 else:
                     nc.vector.tensor_scalar(result[:], sums[h][m][:], bias[:, m : m + 1], 0.0, ADD, MAX)

@@ -41,12 +41,13 @@ def tile_lookup_vg_multanh_relu_kernel(tc, tab, y, w, b, offs, out):
             rows = slice(k * P, (k + 1) * P)
             gates.append(held.tile([P, S], F32, name=f"gates{k}"))
             values.append(held.tile([P, S], F32, name=f"values{k}"))
-            streams.append([held.tile([P, PIECE], F32, name=f"stream{k}_{h}") for h in range(PIECES)])
+            streams.append(held.tile([P, N], F32, name=f"stream{k}"))
             weights.append(held.tile([P, M], BF16, name=f"weights{k}"))
             nc.sync.dma_start(gates[k][:], tab[1, rows, :])
             nc.sync.dma_start(values[k][:], tab[0, rows, :])
-            for h in range(PIECES):
-                nc.sync.dma_start(streams[k][h][:], y[rows, h * PIECE : (h + 1) * PIECE])
+            width = PIECE if k == BLOCKS - 1 else N
+            for c in range(0, N, width):
+                nc.sync.dma_start(streams[k][:, c : c + width], y[rows, c : c + width])
             nc.sync.dma_start(weights[k][:], w[rows, :])
 
         identity = held.tile([32, 32], F32, name="identity")
@@ -64,10 +65,11 @@ def tile_lookup_vg_multanh_relu_kernel(tc, tab, y, w, b, offs, out):
         for k in range(BLOCKS):
             for h in range(PIECES):
                 entries = offsets[:, h * (PIECE // 16) : (h + 1) * (PIECE // 16)]
+                cols = slice(h * PIECE, (h + 1) * PIECE)
                 opened = held.tile([P, PIECE], F32, name=f"opened{k}_{h}")
                 nc.scalar.activation(opened[:], gates[k][:].indirect(entries), TANH)
-                scaled = held.tile([P, PIECE], F32, name=f"scaled{k}_{h}")
-                nc.vector.tensor_tensor(scaled[:], values[k][:].indirect(entries), streams[k][h][:], MULT)
+                scaled = held.tile([P, PIECE], F32, name="scaled")
+                nc.vector.tensor_tensor(scaled[:], values[k][:].indirect(entries), streams[k][:, cols], MULT)
                 x = held.tile([P, PIECE], BF16, name=f"x{k}_{h}")
                 nc.vector.tensor_tensor(x[:], scaled[:], opened[:], MULT)
                 for m in range(OUT_BLOCKS):
@@ -82,7 +84,7 @@ def tile_lookup_vg_multanh_relu_kernel(tc, tab, y, w, b, offs, out):
         for h in range(PIECES):
             for m in range(OUT_BLOCKS):
                 result = held.tile([P, PIECE], F32, name=f"result{h}_{m}")
-                if h == 0 or m % 2 == 1:
+                if m % 2 == 0 or (h == 0 and m < OUT_BLOCKS - 1):
                     nc.scalar.activation(result[:], sums[h][m][:], RELU, bias=bias[:, m : m + 1])
                 else:
                     nc.vector.tensor_scalar(result[:], sums[h][m][:], bias[:, m : m + 1], 0.0, ADD, MAX)

@@ -30,11 +30,9 @@ def tile_lookup_vg_multanh_relu_kernel(tc, tab, y, w, b, offs, out):
         tc.psum_pool(name="psum", bufs=1) as psum,
     ):
         offsets = held.tile([P, N // 16], U16, name="offsets")
-        nc.sync.dma_start(offsets[:], offs)
 
         bias_rows = held.tile([32, P], F32, name="bias_rows")
         nc.vector.memset(bias_rows[:], 0.0)
-        nc.sync.dma_start(bias_rows[0:OUT_BLOCKS, :], b.rearrange("(t p) o -> t (p o)", p=P))
 
         gates, values, streams, weights = [], [], [], []
         for k in range(BLOCKS):
@@ -44,11 +42,15 @@ def tile_lookup_vg_multanh_relu_kernel(tc, tab, y, w, b, offs, out):
             streams.append(held.tile([P, N], F32, name=f"stream{k}"))
             weights.append(held.tile([P, M], BF16, name=f"weights{k}"))
             nc.sync.dma_start(gates[k][:], tab[1, rows, :])
+            if k == 0:
+                nc.sync.dma_start(offsets[:], offs)
             nc.sync.dma_start(values[k][:], tab[0, rows, :])
             width = PIECE if k == BLOCKS - 1 else N
             for c in range(0, N, width):
                 nc.sync.dma_start(streams[k][:, c : c + width], y[rows, c : c + width])
             nc.sync.dma_start(weights[k][:], w[rows, :])
+            if k == 0:
+                nc.sync.dma_start(bias_rows[0:OUT_BLOCKS, :], b.rearrange("(t p) o -> t (p o)", p=P))
 
         identity = held.tile([32, 32], F32, name="identity")
         make_identity(nc, identity[:])

import concourse.mybir as mybir
from concourse.masks import make_identity

F32 = mybir.dt.float32
BF16 = mybir.dt.bfloat16
U16 = mybir.dt.uint16
ADD = mybir.AluOpType.add
MAX = mybir.AluOpType.max
MULT = mybir.AluOpType.mult
TANH = mybir.ActivationFunctionType.Tanh
RELU = mybir.ActivationFunctionType.Relu

P = 128
K = 512
S = 2048
N = 1024
M = 512
PIECE = 512
BLOCKS = K // P
PIECES = N // PIECE
OUT_BLOCKS = M // P

FLOPS = 2 * K * M * N


def tile_lookup_vg_multanh_relu_kernel(tc, tab, y, w, b, offs, out):
    nc = tc.nc
    with (
        tc.tile_pool(name="held", bufs=1) as held,
        tc.psum_pool(name="psum", bufs=1) as psum,
    ):
        offsets = held.tile([P, N // 16], U16, name="offsets")

        bias_rows = held.tile([32, P], F32, name="bias_rows")
        nc.vector.memset(bias_rows[:], 0.0)

        gates, values, streams, weights = [], [], [], []
        for k in range(BLOCKS):
            rows = slice(k * P, (k + 1) * P)
            gates.append(held.tile([P, S], F32, name=f"gates{k}"))
            values.append(held.tile([P, S], F32, name=f"values{k}"))
            streams.append(held.tile([P, N], F32, name=f"stream{k}"))
            weights.append(held.tile([P, M], BF16, name=f"weights{k}"))
            nc.sync.dma_start(gates[k][:], tab[1, rows, :])
            if k == 0:
                nc.sync.dma_start(offsets[:], offs)
            nc.sync.dma_start(values[k][:], tab[0, rows, :])
            width = PIECE if k == BLOCKS - 1 else N
            for c in range(0, N, width):
                nc.sync.dma_start(streams[k][:, c : c + width], y[rows, c : c + width])
            nc.sync.dma_start(weights[k][:], w[rows, :])
            if k == 0:
                nc.sync.dma_start(bias_rows[0:OUT_BLOCKS, :], b.rearrange("(t p) o -> t (p o)", p=P))

        identity = held.tile([32, 32], F32, name="identity")
        make_identity(nc, identity[:])
        bias_psum = psum.tile([P, PIECE], F32, name="bias_psum", tag="acc0_0")
        nc.tensor.matmul(bias_psum[:, 0:OUT_BLOCKS], bias_rows[:], identity[:, 0:OUT_BLOCKS], start=True, stop=True)
        bias = held.tile([P, OUT_BLOCKS], F32, name="bias")
        nc.vector.tensor_copy(bias[:], bias_psum[:, 0:OUT_BLOCKS])

        sums = [
            [psum.tile([P, PIECE], F32, name=f"acc{h}_{m}", tag=f"acc{h}_{m}") for m in range(OUT_BLOCKS)]
            for h in range(PIECES)
        ]

        for k in range(BLOCKS):
            for h in range(PIECES):
                entries = offsets[:, h * (PIECE // 16) : (h + 1) * (PIECE // 16)]
                cols = slice(h * PIECE, (h + 1) * PIECE)
                opened = held.tile([P, PIECE], F32, name=f"opened{k}_{h}")
                nc.scalar.activation(opened[:], gates[k][:].indirect(entries), TANH)
                scaled = held.tile([P, PIECE], F32, name="scaled")
                nc.vector.tensor_tensor(scaled[:], values[k][:].indirect(entries), streams[k][:, cols], MULT)
                x = held.tile([P, PIECE], BF16, name=f"x{k}_{h}")
                nc.vector.tensor_tensor(x[:], scaled[:], opened[:], MULT)
                for m in range(OUT_BLOCKS):
                    nc.tensor.matmul(
                        sums[h][m][:],
                        weights[k][:, m * P : (m + 1) * P],
                        x[:],
                        start=(k == 0),
                        stop=(k == BLOCKS - 1),
                    )

        for h in range(PIECES):
            for m in range(OUT_BLOCKS):
                result = held.tile([P, PIECE], F32, name=f"result{h}_{m}")
                if m % 2 == 0 or (h == 0 and m < OUT_BLOCKS - 1):
                    nc.scalar.activation(result[:], sums[h][m][:], RELU, bias=bias[:, m : m + 1])
                else:
                    nc.vector.tensor_scalar(result[:], sums[h][m][:], bias[:, m : m + 1], 0.0, ADD, MAX)
                nc.sync.dma_start(out[m * P : (m + 1) * P, h * PIECE : (h + 1) * PIECE], result[:])
